import numpy as np
import ml_dtypes


def mxq(x, axis, fmt="e4m3"):
    dtype, down = {"e4m3": (ml_dtypes.float8_e4m3fn, 7), "e5m2": (ml_dtypes.float8_e5m2, 14)}[fmt]
    v = np.moveaxis(np.asarray(x, np.float32).astype(ml_dtypes.bfloat16).astype(np.float64), axis, -1)
    blocks = v.reshape(v.shape[:-1] + (-1, 32))
    amax = np.abs(blocks).max(-1, keepdims=True)
    byte = np.maximum(np.where(amax > 0, np.frexp(amax)[1] - 1 + 127, 0) - down, 1)
    scale = np.exp2(byte - 127.0)
    codes = (blocks / scale).astype(np.float32).astype(dtype).astype(np.float64)
    return np.moveaxis((codes * scale).reshape(v.shape), -1, axis)


WIDE = False


def mx_kscale(k):
    if not WIDE:
        return np.ones(k)
    levels = np.array([10, -10, 5, -5, 0])
    if k % 512:
        return np.exp2(np.random.permutation(np.resize(levels, k // 32))).repeat(32)
    a = np.empty((k // 512, 16))
    for p in range(k // 512):
        a[p, :8] = np.random.permutation(np.resize(levels, 8))
        for g in range(8):
            far = levels[np.abs(levels - a[p, g]) >= 10]
            a[p, g + 8] = far[np.random.randint(len(far))]
    return np.exp2(a.ravel()).repeat(32)


def f64(x):
    return np.asarray(x).astype(np.float64)


def striped(idx):
    return np.tile(idx.reshape(-1, 16).T, (8, 1)).astype(np.uint16)


def unstriped(offs):
    return offs[:16].T.reshape(-1).astype(np.int64)


K, T, E, C, N = 1024, 512, 4, 256, 128


def by_expert(wq, xq):
    return np.concatenate([wq[e].T @ xq[:, e * C:(e + 1) * C] for e in range(E)], axis=1)


def setup_inputs():
    n = np.random.standard_normal
    s = mx_kscale(K)[:, None]
    first = np.random.permutation(np.repeat(np.arange(E), T // E))
    second = (first + 1 + np.random.permutation(np.repeat(np.arange(E - 1), -(-T // (E - 1)))[:T])) % E
    while np.bincount(second, minlength=E).max() != T // E:
        load = np.bincount(second, minlength=E); hi, lo = int(load.argmax()), int(load.argmin())
        t = np.flatnonzero((second == hi) & (first != lo))[0]; second[t] = lo
    slot_token = np.empty(E * C, np.int64); pos = np.empty((2, T), np.int64); fill = np.zeros(E, np.int64)
    place = np.stack([np.random.permutation(C) for _ in range(E)])
    for r, deal in enumerate((first, second)):
        for t in np.random.permutation(T):
            e = deal[t]; j = e * C + place[e, fill[e]]; fill[e] += 1; slot_token[j] = t; pos[r, t] = j
    g = np.random.uniform(0.2, 0.8, T)
    return {
        "xT": (n((K, T)) * s).astype(np.float32),
        "w": (n((E, K, N)) / np.sqrt(K) / s[None]).astype(np.float32),
        "gate": np.stack([np.tile(g, (N, 1)), np.tile(1.0 - g, (N, 1))]).astype(np.float32),
        "offs": striped(slot_token),
        "pos1": striped(pos[0]),
        "pos2": striped(pos[1]),
    }


def reference(xT, w, gate, offs, pos1, pos2):
    idx = unstriped(offs)
    xq = mxq(f64(xT)[:, idx], 0, "e4m3")
    y = by_expert(mxq(f64(w), 1, "e4m3"), xq)
    return f64(gate[0]) * y[:, unstriped(pos1)] + f64(gate[1]) * y[:, unstriped(pos2)]

@@ -1,0 +1,125 @@
+from contextlib import ExitStack
+
+import concourse.mybir as mybir
+
+K, T, E, C, N = 1024, 512, 4, 256, 128
+FLOPS = 2 * K * E * C * N
+
+F32 = mybir.dt.float32
+BF16 = mybir.dt.bfloat16
+U32 = mybir.dt.uint32
+U16 = mybir.dt.uint16
+U8 = mybir.dt.uint8
+FP8X4 = mybir.dt.float8_e4m3fn_x4
+MULT = mybir.AluOpType.mult
+ADD = mybir.AluOpType.add
+COPY = mybir.ActivationFunctionType.Copy
+
+P = 128
+PASSES = K // 512
+
+
+def tile_routed_moe_kernel(tc, xT, w, gate, offs, pos1, pos2, out):
+    nc = tc.nc
+    with ExitStack() as ctx:
+        lists = ctx.enter_context(tc.tile_pool(name="lists", bufs=1))
+        keep = ctx.enter_context(tc.tile_pool(name="keep", bufs=1))
+        psum = ctx.enter_context(tc.psum_pool(name="psum", bufs=1))
+
+        offs_t = lists.tile([P, E * C // 16], U16, name="offs_t")
+        pos1_t = lists.tile([P, T // 16], U16, name="pos1_t")
+        pos2_t = lists.tile([P, T // 16], U16, name="pos2_t")
+        nc.sync.dma_start(offs_t[:], offs)
+
+        x_view = xT.rearrange("(g p t) n -> g p t n", g=PASSES, p=P, t=4)
+        raw = []
+        for g in range(PASSES):
+            raw.append(keep.tile([P, 4, T], F32, name="raw%d" % g))
+            for h in range(2):
+                nc.sync.dma_start(raw[g][:, 2 * h : 2 * h + 2, :], x_view[g, :, 2 * h : 2 * h + 2, :])
+        w_raw = []
+        for e in range(E):
+            w_raw.append(keep.tile([P, PASSES, 4, N], F32, name="w_raw%d" % e))
+            nc.sync.dma_start(w_raw[e][:], w[e].rearrange("(g p t) n -> p g t n", g=PASSES, p=P, t=4))
+        nc.sync.dma_start(pos1_t[:], pos1)
+        nc.sync.dma_start(pos2_t[:], pos2)
+        gate_t = []
+        for r in range(2):
+            gate_t.append(keep.tile([P, T], F32, name="gate%d" % r))
+            nc.sync.dma_start(gate_t[r][:], gate[r])
+
+        w_codes, w_scales, w_grouped = [], [], []
+        for e in range(E):
+            w_grouped.append(keep.tile([P, PASSES * N * 4], BF16, name="w_grouped%d" % e, align_bytes=64))
+            w_codes.append(keep.tile([P, PASSES * N], U32, name="w_codes%d" % e, align_bytes=64))
+            w_scales.append(keep.tile([P, PASSES * N], U8, name="w_scales%d" % e, align_bytes=64))
+
+        def w_interleave(e):
+            nc.scalar.copy(
+                out=w_grouped[e][:].rearrange("p (g n t) -> p g n t", g=PASSES, t=4),
+                in_=w_raw[e][:].rearrange("p g t n -> p g n t"),
+            )
+
+        def w_quantize(e):
+            nc.vector.quantize_mx(out=w_codes[e][:].bitcast(FP8X4), scales=w_scales[e][:], in_=w_grouped[e][:])
+
+        x_codes = [keep.tile([P, E * C], U32, name="x_codes%d" % g, align_bytes=64) for g in range(PASSES)]
+        x_scales = [keep.tile([P, E * C], U8, name="x_scales%d" % g, align_bytes=64) for g in range(PASSES)]
+        acc = [psum.tile([P, C], F32, name="acc%d" % e) for e in range(E)]
+        y_sb = keep.tile([P, E * C], F32, name="y_sb")
+
+        grouped = {}
+        for g in range(PASSES):
+            for e in range(E):
+                grouped[g, e] = keep.tile([P, C, 4], BF16, name="grouped%d%d" % (g, e), align_bytes=64)
+
+        def gather(g, e, t):
+            nc.vector.tensor_copy(grouped[g, e][:, :, t], raw[g][:, t, :].indirect(offs_t[:, 16 * e : 16 * (e + 1)]))
+
+        def quantize(g, e):
+            cols = slice(e * C, (e + 1) * C)
+            nc.vector.quantize_mx(
+                out=x_codes[g][:, cols].bitcast(FP8X4),
+                scales=x_scales[g][:, cols],
+                in_=grouped[g, e][:].rearrange("p n t -> p (n t)"),
+            )
+
+        def multiply(g, e):
+            cols = slice(e * C, (e + 1) * C)
+            wcols = slice(g * N, (g + 1) * N)
+            nc.tensor.matmul_mx(
+                out=acc[e][:],
+                lhsT=w_codes[e][:, wcols].bitcast(FP8X4),
+                lhsT_scale=w_scales[e][:, wcols],
+                rhs=x_codes[g][:, cols].bitcast(FP8X4),
+                rhs_scale=x_scales[g][:, cols],
+                start=(g == 0),
+                stop=(g == PASSES - 1),
+            )
+
+        def finish(g, e):
+            quantize(g, e)
+            if g == 0:
+                w_quantize(e)
+            multiply(g, e)
+            if g == PASSES - 1:
+                nc.scalar.copy(out=y_sb[:, e * C : (e + 1) * C], in_=acc[e][:])
+
+        for e in range(E):
+            w_interleave(e)
+        for g in range(PASSES):
+            for e in range(E):
+                gather(g, e, 0)
+                if (g, e) != (0, 0):
+                    finish(*((g, e - 1) if e else (g - 1, E - 1)))
+                for t in range(1, 4):
+                    gather(g, e, t)
+        finish(PASSES - 1, E - 1)
+
+        first = keep.tile([P, T], F32, name="first")
+        second = keep.tile([P, T], F32, name="second")
+        nc.vector.tensor_tensor(first[:], y_sb[:].indirect(pos1_t[:]), gate_t[0][:], MULT)
+        nc.vector.tensor_tensor(second[:], y_sb[:].indirect(pos2_t[:]), gate_t[1][:], MULT)
+        result = keep.tile([P, T], F32, name="result")
+        nc.vector.tensor_tensor(result[:], first[:], second[:], ADD)
+        nc.sync.dma_start(out, result[:])

@@ -18,12 +18,15 @@ COPY = mybir.ActivationFunctionType.Copy
 P = 128
 PASSES = K // 512
 
+V_SLOTS = [256,0,0,0]
+
 
 def tile_routed_moe_kernel(tc, xT, w, gate, offs, pos1, pos2, out):
     nc = tc.nc
     with ExitStack() as ctx:
         lists = ctx.enter_context(tc.tile_pool(name="lists", bufs=1))
         keep = ctx.enter_context(tc.tile_pool(name="keep", bufs=1))
+        ring = ctx.enter_context(tc.tile_pool(name="ring", bufs=3))
         psum = ctx.enter_context(tc.psum_pool(name="psum", bufs=1))
 
         offs_t = lists.tile([P, E * C // 16], U16, name="offs_t")
@@ -35,8 +38,8 @@ def tile_routed_moe_kernel(tc, xT, w, gate, offs, pos1, pos2, out):
         raw = []
         for g in range(PASSES):
             raw.append(keep.tile([P, 4, T], F32, name="raw%d" % g))
-            for h in range(2):
-                nc.sync.dma_start(raw[g][:, 2 * h : 2 * h + 2, :], x_view[g, :, 2 * h : 2 * h + 2, :])
+            for t in range(4):
+                nc.sync.dma_start(raw[g][:, t, :], x_view[g, :, t, :])
         w_raw = []
         for e in range(E):
             w_raw.append(keep.tile([P, PASSES, 4, N], F32, name="w_raw%d" % e))
@@ -48,73 +51,66 @@ def tile_routed_moe_kernel(tc, xT, w, gate, offs, pos1, pos2, out):
             gate_t.append(keep.tile([P, T], F32, name="gate%d" % r))
             nc.sync.dma_start(gate_t[r][:], gate[r])
 
-        w_codes, w_scales, w_grouped = [], [], []
+        xb = [keep.tile([P, 4, T], BF16, name="xb%d" % g) for g in range(PASSES)]
+        for g in range(PASSES):
+            for t in range(4):
+                nc.vector.tensor_copy(out=xb[g][:, t, :], in_=raw[g][:, t, :])
+
+        w_codes, w_scales = [], []
         for e in range(E):
-            w_grouped.append(keep.tile([P, PASSES * N * 4], BF16, name="w_grouped%d" % e, align_bytes=64))
+            w_grouped = keep.tile([P, PASSES * N * 4], BF16, name="w_grouped%d" % e, align_bytes=64)
             w_codes.append(keep.tile([P, PASSES * N], U32, name="w_codes%d" % e, align_bytes=64))
             w_scales.append(keep.tile([P, PASSES * N], U8, name="w_scales%d" % e, align_bytes=64))
-
-        def w_interleave(e):
-            nc.scalar.copy(
-                out=w_grouped[e][:].rearrange("p (g n t) -> p g n t", g=PASSES, t=4),
+            nc.vector.tensor_copy(
+                out=w_grouped[:].rearrange("p (g n t) -> p g n t", g=PASSES, t=4),
                 in_=w_raw[e][:].rearrange("p g t n -> p g n t"),
             )
-
-        def w_quantize(e):
-            nc.vector.quantize_mx(out=w_codes[e][:].bitcast(FP8X4), scales=w_scales[e][:], in_=w_grouped[e][:])
+            nc.vector.quantize_mx(out=w_codes[e][:].bitcast(FP8X4), scales=w_scales[e][:], in_=w_grouped[:])
 
         x_codes = [keep.tile([P, E * C], U32, name="x_codes%d" % g, align_bytes=64) for g in range(PASSES)]
         x_scales = [keep.tile([P, E * C], U8, name="x_scales%d" % g, align_bytes=64) for g in range(PASSES)]
         acc = [psum.tile([P, C], F32, name="acc%d" % e) for e in range(E)]
         y_sb = keep.tile([P, E * C], F32, name="y_sb")
 
-        grouped = {}
         for g in range(PASSES):
             for e in range(E):
-                grouped[g, e] = keep.tile([P, C, 4], BF16, name="grouped%d%d" % (g, e), align_bytes=64)
-
-        def gather(g, e, t):
-            nc.vector.tensor_copy(grouped[g, e][:, :, t], raw[g][:, t, :].indirect(offs_t[:, 16 * e : 16 * (e + 1)]))
-
-        def quantize(g, e):
-            cols = slice(e * C, (e + 1) * C)
-            nc.vector.quantize_mx(
-                out=x_codes[g][:, cols].bitcast(FP8X4),
-                scales=x_scales[g][:, cols],
-                in_=grouped[g, e][:].rearrange("p n t -> p (n t)"),
-            )
-
-        def multiply(g, e):
-            cols = slice(e * C, (e + 1) * C)
-            wcols = slice(g * N, (g + 1) * N)
-            nc.tensor.matmul_mx(
-                out=acc[e][:],
-                lhsT=w_codes[e][:, wcols].bitcast(FP8X4),
-                lhsT_scale=w_scales[e][:, wcols],
-                rhs=x_codes[g][:, cols].bitcast(FP8X4),
-                rhs_scale=x_scales[g][:, cols],
-                start=(g == 0),
-                stop=(g == PASSES - 1),
-            )
-
-        def finish(g, e):
-            quantize(g, e)
-            if g == 0:
-                w_quantize(e)
-            multiply(g, e)
-            if g == PASSES - 1:
-                nc.scalar.copy(out=y_sb[:, e * C : (e + 1) * C], in_=acc[e][:])
-
-        for e in range(E):
-            w_interleave(e)
-        for g in range(PASSES):
-            for e in range(E):
-                gather(g, e, 0)
-                if (g, e) != (0, 0):
-                    finish(*((g, e - 1) if e else (g - 1, E - 1)))
-                for t in range(1, 4):
-                    gather(g, e, t)
-        finish(PASSES - 1, E - 1)
+                cut = V_SLOTS[e]
+                halves = ring.tile([P, 2, 2 * C], BF16, name="halves")
+                for t in range(4):
+                    plane = halves[:, t // 2, :].rearrange("p (n i) -> p n i", i=2)
+                    first_col = e * C // 16
+                    if cut > 0:
+                        nc.vector.tensor_copy(
+                            plane[:, 0:cut, t % 2],
+                            raw[g][:, t, :].indirect(offs_t[:, first_col : first_col + cut // 16]),
+                        )
+                    if cut < C:
+                        nc.scalar.activation(
+                            plane[:, cut:C, t % 2],
+                            xb[g][:, t, :].indirect(offs_t[:, first_col + cut // 16 : first_col + C // 16]),
+                            COPY,
+                        )
+                grouped = ring.tile([P, C * 4], BF16, name="grouped", align_bytes=64)
+                nc.vector.tensor_copy(
+                    out=grouped[:].bitcast(F32).rearrange("p (n u) -> p n u", u=2),
+                    in_=halves[:].bitcast(F32).rearrange("p u n -> p n u"),
+                )
+                cols = slice(e * C, (e + 1) * C)
+                wcols = slice(g * N, (g + 1) * N)
+                nc.vector.quantize_mx(
+                    out=x_codes[g][:, cols].bitcast(FP8X4), scales=x_scales[g][:, cols], in_=grouped[:]
+                )
+                nc.tensor.matmul_mx(
+                    out=acc[e][:],
+                    lhsT=w_codes[e][:, wcols].bitcast(FP8X4),
+                    lhsT_scale=w_scales[e][:, wcols],
+                    rhs=x_codes[g][:, cols].bitcast(FP8X4),
+                    rhs_scale=x_scales[g][:, cols],
+                    start=(g == 0),
+                    stop=(g == PASSES - 1),
+                )
+                if g == PASSES - 1:
+                    nc.scalar.copy(out=y_sb[:, cols], in_=acc[e][:])
 
         first = keep.tile([P, T], F32, name="first")
         second = keep.tile([P, T], F32, name="second")

@@ -18,7 +18,9 @@ COPY = mybir.ActivationFunctionType.Copy
 P = 128
 PASSES = K // 512
 
-V_SLOTS = [256,0,0,0]
+
+def on_vector(g, e, u):
+    return e == 0 or (g == 0 and e == 1 and u == 1)
 
 
 def tile_routed_moe_kernel(tc, xT, w, gate, offs, pos1, pos2, out):
@@ -26,13 +28,17 @@ def tile_routed_moe_kernel(tc, xT, w, gate, offs, pos1, pos2, out):
     with ExitStack() as ctx:
         lists = ctx.enter_context(tc.tile_pool(name="lists", bufs=1))
         keep = ctx.enter_context(tc.tile_pool(name="keep", bufs=1))
-        ring = ctx.enter_context(tc.tile_pool(name="ring", bufs=3))
         psum = ctx.enter_context(tc.psum_pool(name="psum", bufs=1))
 
         offs_t = lists.tile([P, E * C // 16], U16, name="offs_t")
         pos1_t = lists.tile([P, T // 16], U16, name="pos1_t")
         pos2_t = lists.tile([P, T // 16], U16, name="pos2_t")
         nc.sync.dma_start(offs_t[:], offs)
+
+        warm_in = keep.tile([P, 1], F32, name="warm_in")
+        warm_out = keep.tile([P, 1], F32, name="warm_out")
+        nc.vector.memset(warm_in[:], 0.0)
+        nc.scalar.activation(warm_out[:], warm_in[:], COPY)
 
         x_view = xT.rearrange("(g p t) n -> g p t n", g=PASSES, p=P, t=4)
         raw = []
@@ -51,10 +57,11 @@ def tile_routed_moe_kernel(tc, xT, w, gate, offs, pos1, pos2, out):
             gate_t.append(keep.tile([P, T], F32, name="gate%d" % r))
             nc.sync.dma_start(gate_t[r][:], gate[r])
 
-        xb = [keep.tile([P, 4, T], BF16, name="xb%d" % g) for g in range(PASSES)]
-        for g in range(PASSES):
-            for t in range(4):
-                nc.vector.tensor_copy(out=xb[g][:, t, :], in_=raw[g][:, t, :])
+        xb = [keep.tile([P, 4, T], BF16, name="xb0"), keep.tile([P, 4, T], BF16, name="xb1", tag="late")]
+        for t in range(4):
+            nc.gpsimd.tensor_scalar(xb[0][:, t, :], raw[0][:, t, :], 1.0, 0.0, MULT, ADD)
+        for u in range(2):
+            nc.gpsimd.tensor_scalar(xb[1][:, 2 * u : 2 * u + 2, :], raw[1][:, 2 * u : 2 * u + 2, :], 1.0, 0.0, MULT, ADD)
 
         w_codes, w_scales = [], []
         for e in range(E):
@@ -62,35 +69,28 @@ def tile_routed_moe_kernel(tc, xT, w, gate, offs, pos1, pos2, out):
             w_codes.append(keep.tile([P, PASSES * N], U32, name="w_codes%d" % e, align_bytes=64))
             w_scales.append(keep.tile([P, PASSES * N], U8, name="w_scales%d" % e, align_bytes=64))
             nc.vector.tensor_copy(
-                out=w_grouped[:].rearrange("p (g n t) -> p g n t", g=PASSES, t=4),
-                in_=w_raw[e][:].rearrange("p g t n -> p g n t"),
+                out=w_grouped[:].rearrange("p (g c i t) -> p g c t i", g=PASSES, i=4, t=4),
+                in_=w_raw[e][:].rearrange("p g t (c i) -> p g c t i", i=4),
             )
             nc.vector.quantize_mx(out=w_codes[e][:].bitcast(FP8X4), scales=w_scales[e][:], in_=w_grouped[:])
 
         x_codes = [keep.tile([P, E * C], U32, name="x_codes%d" % g, align_bytes=64) for g in range(PASSES)]
         x_scales = [keep.tile([P, E * C], U8, name="x_scales%d" % g, align_bytes=64) for g in range(PASSES)]
         acc = [psum.tile([P, C], F32, name="acc%d" % e) for e in range(E)]
-        y_sb = keep.tile([P, E * C], F32, name="y_sb")
+        y_sb = keep.tile([P, E * C], F32, name="y_sb", tag="late")
 
         for g in range(PASSES):
             for e in range(E):
-                cut = V_SLOTS[e]
-                halves = ring.tile([P, 2, 2 * C], BF16, name="halves")
+                halves = keep.tile([P, 2, 2 * C], BF16, name="halves%d_%d" % (g, e))
                 for t in range(4):
                     plane = halves[:, t // 2, :].rearrange("p (n i) -> p n i", i=2)
                     first_col = e * C // 16
-                    if cut > 0:
-                        nc.vector.tensor_copy(
-                            plane[:, 0:cut, t % 2],
-                            raw[g][:, t, :].indirect(offs_t[:, first_col : first_col + cut // 16]),
-                        )
-                    if cut < C:
-                        nc.scalar.activation(
-                            plane[:, cut:C, t % 2],
-                            xb[g][:, t, :].indirect(offs_t[:, first_col + cut // 16 : first_col + C // 16]),
-                            COPY,
-                        )
-                grouped = ring.tile([P, C * 4], BF16, name="grouped", align_bytes=64)
+                    picked = offs_t[:, first_col : first_col + C // 16]
+                    if on_vector(g, e, t // 2):
+                        nc.vector.tensor_copy(plane[:, :, t % 2], raw[g][:, t, :].indirect(picked))
+                    else:
+                        nc.scalar.activation(plane[:, :, t % 2], xb[g][:, t, :].indirect(picked), COPY)
+                grouped = keep.tile([P, C * 4], BF16, name="grouped%d_%d" % (g, e), align_bytes=64)
                 nc.vector.tensor_copy(
                     out=grouped[:].bitcast(F32).rearrange("p (n u) -> p n u", u=2),
                     in_=halves[:].bitcast(F32).rearrange("p u n -> p n u"),

@@ -43,7 +43,7 @@ def tile_routed_moe_kernel(tc, xT, w, gate, offs, pos1, pos2, out):
         x_view = xT.rearrange("(g p t) n -> g p t n", g=PASSES, p=P, t=4)
         raw = []
         for g in range(PASSES):
-            raw.append(keep.tile([P, 4, T], F32, name="raw%d" % g))
+            raw.append(keep.tile([P, 4, T], F32, name="raw%d" % g, tag="raw%d" % g, align_bytes=64))
             for t in range(4):
                 nc.sync.dma_start(raw[g][:, t, :], x_view[g, :, t, :])
         w_raw = []
@@ -68,16 +68,27 @@ def tile_routed_moe_kernel(tc, xT, w, gate, offs, pos1, pos2, out):
             w_grouped = keep.tile([P, PASSES * N * 4], BF16, name="w_grouped%d" % e, align_bytes=64)
             w_codes.append(keep.tile([P, PASSES * N], U32, name="w_codes%d" % e, align_bytes=64))
             w_scales.append(keep.tile([P, PASSES * N], U8, name="w_scales%d" % e, align_bytes=64))
-            nc.vector.tensor_copy(
-                out=w_grouped[:].rearrange("p (g c i t) -> p g c t i", g=PASSES, i=4, t=4),
-                in_=w_raw[e][:].rearrange("p g t (c i) -> p g c t i", i=4),
-            )
+            if e == 0:
+                nc.gpsimd.tensor_scalar(
+                    w_grouped[:].rearrange("p (g n t) -> p g n t", g=PASSES, t=4),
+                    w_raw[e][:].rearrange("p g t n -> p g n t"),
+                    1.0,
+                    0.0,
+                    MULT,
+                    ADD,
+                )
+            else:
+                nc.vector.tensor_copy(
+                    out=w_grouped[:].rearrange("p (g c i t) -> p g c t i", g=PASSES, i=4, t=4),
+                    in_=w_raw[e][:].rearrange("p g t (c i) -> p g c t i", i=4),
+                )
             nc.vector.quantize_mx(out=w_codes[e][:].bitcast(FP8X4), scales=w_scales[e][:], in_=w_grouped[:])
 
         x_codes = [keep.tile([P, E * C], U32, name="x_codes%d" % g, align_bytes=64) for g in range(PASSES)]
         x_scales = [keep.tile([P, E * C], U8, name="x_scales%d" % g, align_bytes=64) for g in range(PASSES)]
         acc = [psum.tile([P, C], F32, name="acc%d" % e) for e in range(E)]
         y_sb = keep.tile([P, E * C], F32, name="y_sb", tag="late")
+        early = keep.tile([P, 2, C * 4], BF16, name="early", tag="raw1", align_bytes=64)
 
         for g in range(PASSES):
             for e in range(E):
@@ -90,15 +101,18 @@ def tile_routed_moe_kernel(tc, xT, w, gate, offs, pos1, pos2, out):
                         nc.vector.tensor_copy(plane[:, :, t % 2], raw[g][:, t, :].indirect(picked))
                     else:
                         nc.scalar.activation(plane[:, :, t % 2], xb[g][:, t, :].indirect(picked), COPY)
-                grouped = keep.tile([P, C * 4], BF16, name="grouped%d_%d" % (g, e), align_bytes=64)
+                if g == 0 and e < 2:
+                    grouped = early[:, e, :]
+                else:
+                    grouped = keep.tile([P, C * 4], BF16, name="grouped%d_%d" % (g, e), align_bytes=64)[:]
                 nc.vector.tensor_copy(
-                    out=grouped[:].bitcast(F32).rearrange("p (n u) -> p n u", u=2),
+                    out=grouped.bitcast(F32).rearrange("p (n u) -> p n u", u=2),
                     in_=halves[:].bitcast(F32).rearrange("p u n -> p n u"),
                 )
                 cols = slice(e * C, (e + 1) * C)
                 wcols = slice(g * N, (g + 1) * N)
                 nc.vector.quantize_mx(
-                    out=x_codes[g][:, cols].bitcast(FP8X4), scales=x_scales[g][:, cols], in_=grouped[:]
+                    out=x_codes[g][:, cols].bitcast(FP8X4), scales=x_scales[g][:, cols], in_=grouped
                 )
                 nc.tensor.matmul_mx(
                     out=acc[e][:],

@@ -19,6 +19,9 @@ P = 128
 PASSES = K // 512
 
 
+PARTS = [1, 1, 1, 2]
+
+
 def on_vector(g, e, u):
     return e == 0 or (g == 0 and e == 1 and u == 1)
 
@@ -58,7 +61,8 @@ def tile_routed_moe_kernel(tc, xT, w, gate, offs, pos1, pos2, out):
             nc.sync.dma_start(gate_t[r][:], gate[r])
 
         xb = [keep.tile([P, 4, T], BF16, name="xb0"), keep.tile([P, 4, T], BF16, name="xb1", tag="late")]
-        for t in range(4):
+        nc.vector.tensor_copy(out=xb[0][:, 0, :], in_=raw[0][:, 0, :])
+        for t in range(1, 4):
             nc.gpsimd.tensor_scalar(xb[0][:, t, :], raw[0][:, t, :], 1.0, 0.0, MULT, ADD)
         for u in range(2):
             nc.gpsimd.tensor_scalar(xb[1][:, 2 * u : 2 * u + 2, :], raw[1][:, 2 * u : 2 * u + 2, :], 1.0, 0.0, MULT, ADD)
@@ -86,50 +90,60 @@ def tile_routed_moe_kernel(tc, xT, w, gate, offs, pos1, pos2, out):
 
         x_codes = [keep.tile([P, E * C], U32, name="x_codes%d" % g, align_bytes=64) for g in range(PASSES)]
         x_scales = [keep.tile([P, E * C], U8, name="x_scales%d" % g, align_bytes=64) for g in range(PASSES)]
-        acc = [psum.tile([P, C], F32, name="acc%d" % e) for e in range(E)]
+        acc = [[psum.tile([P, C // PARTS[e]], F32, name="acc%d_%d" % (e, h)) for h in range(PARTS[e])] for e in range(E)]
         y_sb = keep.tile([P, E * C], F32, name="y_sb", tag="late")
         early = keep.tile([P, 2, C * 4], BF16, name="early", tag="raw1", align_bytes=64)
 
         for g in range(PASSES):
             for e in range(E):
+                parts = PARTS[e] if g == PASSES - 1 else 1
+                width = C // parts
                 halves = keep.tile([P, 2, 2 * C], BF16, name="halves%d_%d" % (g, e))
-                for t in range(4):
-                    plane = halves[:, t // 2, :].rearrange("p (n i) -> p n i", i=2)
-                    first_col = e * C // 16
-                    picked = offs_t[:, first_col : first_col + C // 16]
-                    if on_vector(g, e, t // 2):
-                        nc.vector.tensor_copy(plane[:, :, t % 2], raw[g][:, t, :].indirect(picked))
+                for u in range(2):
+                    for h in range(parts if u == 1 else 1):
+                        n = width if u == 1 else C
+                        first_col = (e * C + h * n) // 16
+                        picked = offs_t[:, first_col : first_col + n // 16]
+                        for t in (2 * u, 2 * u + 1):
+                            plane = halves[:, u, :].rearrange("p (n i) -> p n i", i=2)[:, h * n : (h + 1) * n, t % 2]
+                            if on_vector(g, e, u):
+                                nc.vector.tensor_copy(plane, raw[g][:, t, :].indirect(picked))
+                            else:
+                                nc.scalar.activation(plane, xb[g][:, t, :].indirect(picked), COPY)
+                for h in range(parts):
+                    if g == 0 and e < 2:
+                        grouped = early[:, e, :]
                     else:
-                        nc.scalar.activation(plane[:, :, t % 2], xb[g][:, t, :].indirect(picked), COPY)
-                if g == 0 and e < 2:
-                    grouped = early[:, e, :]
-                else:
-                    grouped = keep.tile([P, C * 4], BF16, name="grouped%d_%d" % (g, e), align_bytes=64)[:]
-                nc.vector.tensor_copy(
-                    out=grouped.bitcast(F32).rearrange("p (n u) -> p n u", u=2),
-                    in_=halves[:].bitcast(F32).rearrange("p u n -> p n u"),
-                )
-                cols = slice(e * C, (e + 1) * C)
+                        grouped = keep.tile([P, width * 4], BF16, name="grouped%d_%d_%d" % (g, e, h), align_bytes=64)[:]
+                    nc.vector.tensor_copy(
+                        out=grouped.bitcast(F32).rearrange("p (n u) -> p n u", u=2),
+                        in_=halves[:].bitcast(F32)[:, :, h * width : (h + 1) * width].rearrange("p u n -> p n u"),
+                    )
+                    cols = slice(e * C + h * width, e * C + (h + 1) * width)
+                    nc.vector.quantize_mx(
+                        out=x_codes[g][:, cols].bitcast(FP8X4), scales=x_scales[g][:, cols], in_=grouped
+                    )
                 wcols = slice(g * N, (g + 1) * N)
-                nc.vector.quantize_mx(
-                    out=x_codes[g][:, cols].bitcast(FP8X4), scales=x_scales[g][:, cols], in_=grouped
-                )
-                nc.tensor.matmul_mx(
-                    out=acc[e][:],
-                    lhsT=w_codes[e][:, wcols].bitcast(FP8X4),
-                    lhsT_scale=w_scales[e][:, wcols],
-                    rhs=x_codes[g][:, cols].bitcast(FP8X4),
-                    rhs_scale=x_scales[g][:, cols],
-                    start=(g == 0),
-                    stop=(g == PASSES - 1),
-                )
-                if g == PASSES - 1:
-                    nc.scalar.copy(out=y_sb[:, cols], in_=acc[e][:])
+                for h in range(PARTS[e]):
+                    cols = slice(e * C + h * (C // PARTS[e]), e * C + (h + 1) * (C // PARTS[e]))
+                    nc.tensor.matmul_mx(
+                        out=acc[e][h][:],
+                        lhsT=w_codes[e][:, wcols].bitcast(FP8X4),
+                        lhsT_scale=w_scales[e][:, wcols],
+                        rhs=x_codes[g][:, cols].bitcast(FP8X4),
+                        rhs_scale=x_scales[g][:, cols],
+                        start=(g == 0),
+                        stop=(g == PASSES - 1),
+                    )
+                    if g == PASSES - 1:
+                        nc.scalar.copy(out=y_sb[:, cols], in_=acc[e][h][:])
 
         first = keep.tile([P, T], F32, name="first")
         second = keep.tile([P, T], F32, name="second")
         nc.vector.tensor_tensor(first[:], y_sb[:].indirect(pos1_t[:]), gate_t[0][:], MULT)
         nc.vector.tensor_tensor(second[:], y_sb[:].indirect(pos2_t[:]), gate_t[1][:], MULT)
         result = keep.tile([P, T], F32, name="result")
-        nc.vector.tensor_tensor(result[:], first[:], second[:], ADD)
-        nc.sync.dma_start(out, result[:])
+        for h, queue in enumerate((nc.sync, nc.scalar)):
+            cols = slice(h * T // 2, (h + 1) * T // 2)
+            nc.vector.tensor_tensor(result[:, cols], first[:, cols], second[:, cols], ADD)
+            queue.dma_start(out[:, cols], result[:, cols])

@@ -18,7 +18,7 @@ COPY = mybir.ActivationFunctionType.Copy
 P = 128
 PASSES = K // 512
 
-
+UNITS = [(0, (0, 1), 1), (0, (2, 3), 1), (1, (0,), 1), (1, (1,), 1), (1, (2,), 1), (1, (3,), 2)]
 PARTS = [1, 1, 1, 2]
 
 
@@ -50,9 +50,13 @@ def tile_routed_moe_kernel(tc, xT, w, gate, offs, pos1, pos2, out):
             for t in range(4):
                 nc.sync.dma_start(raw[g][:, t, :], x_view[g, :, t, :])
         w_raw = []
-        for e in range(E):
-            w_raw.append(keep.tile([P, PASSES, 4, N], F32, name="w_raw%d" % e))
-            nc.sync.dma_start(w_raw[e][:], w[e].rearrange("(g p t) n -> p g t n", g=PASSES, p=P, t=4))
+        for h in range(E // 2):
+            w_raw.append(keep.tile([P, 2 * PASSES, 4, N], F32, name="w_raw%d" % h))
+            for j in range(2):
+                nc.sync.dma_start(
+                    w_raw[h][:, j * PASSES : (j + 1) * PASSES, :, :],
+                    w[2 * h + j].rearrange("(g p t) n -> p g t n", g=PASSES, p=P, t=4),
+                )
         nc.sync.dma_start(pos1_t[:], pos1)
         nc.sync.dma_start(pos2_t[:], pos2)
         gate_t = []
@@ -67,69 +71,76 @@ def tile_routed_moe_kernel(tc, xT, w, gate, offs, pos1, pos2, out):
         for u in range(2):
             nc.gpsimd.tensor_scalar(xb[1][:, 2 * u : 2 * u + 2, :], raw[1][:, 2 * u : 2 * u + 2, :], 1.0, 0.0, MULT, ADD)
 
+        WE = PASSES * N
         w_codes, w_scales = [], []
-        for e in range(E):
-            w_grouped = keep.tile([P, PASSES * N * 4], BF16, name="w_grouped%d" % e, align_bytes=64)
-            w_codes.append(keep.tile([P, PASSES * N], U32, name="w_codes%d" % e, align_bytes=64))
-            w_scales.append(keep.tile([P, PASSES * N], U8, name="w_scales%d" % e, align_bytes=64))
-            if e == 0:
+        for h in range(E // 2):
+            w_grouped = keep.tile([P, 2 * WE * 4], BF16, name="w_grouped%d" % h, align_bytes=64)
+            w_codes.append(keep.tile([P, 2 * WE], U32, name="w_codes%d" % h, align_bytes=64))
+            w_scales.append(keep.tile([P, 2 * WE], U8, name="w_scales%d" % h, align_bytes=64))
+            if h == 0:
                 nc.gpsimd.tensor_scalar(
-                    w_grouped[:].rearrange("p (g n t) -> p g n t", g=PASSES, t=4),
-                    w_raw[e][:].rearrange("p g t n -> p g n t"),
+                    w_grouped[:, 0 : WE * 4].rearrange("p (g n t) -> p g n t", g=PASSES, t=4),
+                    w_raw[h][:, 0:PASSES, :, :].rearrange("p g t n -> p g n t"),
                     1.0,
                     0.0,
                     MULT,
                     ADD,
                 )
+                nc.vector.tensor_copy(
+                    out=w_grouped[:, WE * 4 : 2 * WE * 4].rearrange("p (g c i t) -> p g c t i", g=PASSES, i=4, t=4),
+                    in_=w_raw[h][:, PASSES : 2 * PASSES, :, :].rearrange("p g t (c i) -> p g c t i", i=4),
+                )
             else:
                 nc.vector.tensor_copy(
-                    out=w_grouped[:].rearrange("p (g c i t) -> p g c t i", g=PASSES, i=4, t=4),
-                    in_=w_raw[e][:].rearrange("p g t (c i) -> p g c t i", i=4),
+                    out=w_grouped[:].rearrange("p (g c i t) -> p g c t i", g=2 * PASSES, i=4, t=4),
+                    in_=w_raw[h][:].rearrange("p g t (c i) -> p g c t i", i=4),
                 )
-            nc.vector.quantize_mx(out=w_codes[e][:].bitcast(FP8X4), scales=w_scales[e][:], in_=w_grouped[:])
+            nc.vector.quantize_mx(out=w_codes[h][:].bitcast(FP8X4), scales=w_scales[h][:], in_=w_grouped[:])
 
         x_codes = [keep.tile([P, E * C], U32, name="x_codes%d" % g, align_bytes=64) for g in range(PASSES)]
         x_scales = [keep.tile([P, E * C], U8, name="x_scales%d" % g, align_bytes=64) for g in range(PASSES)]
         acc = [[psum.tile([P, C // PARTS[e]], F32, name="acc%d_%d" % (e, h)) for h in range(PARTS[e])] for e in range(E)]
         y_sb = keep.tile([P, E * C], F32, name="y_sb", tag="late")
-        early = keep.tile([P, 2, C * 4], BF16, name="early", tag="raw1", align_bytes=64)
 
-        for g in range(PASSES):
-            for e in range(E):
-                parts = PARTS[e] if g == PASSES - 1 else 1
-                width = C // parts
-                halves = keep.tile([P, 2, 2 * C], BF16, name="halves%d_%d" % (g, e))
+        for k, (g, experts, parts) in enumerate(UNITS):
+            slots = C * len(experts)
+            width = slots // parts
+            base = experts[0] * C
+            halves = keep.tile([P, 2, 2 * slots], BF16, name="halves%d" % k)
+            for j, e in enumerate(experts):
                 for u in range(2):
                     for h in range(parts if u == 1 else 1):
-                        n = width if u == 1 else C
+                        n = C // parts if u == 1 else C
                         first_col = (e * C + h * n) // 16
                         picked = offs_t[:, first_col : first_col + n // 16]
                         for t in (2 * u, 2 * u + 1):
-                            plane = halves[:, u, :].rearrange("p (n i) -> p n i", i=2)[:, h * n : (h + 1) * n, t % 2]
+                            plane = halves[:, u, :].rearrange("p (n i) -> p n i", i=2)
+                            plane = plane[:, j * C + h * n : j * C + (h + 1) * n, t % 2]
                             if on_vector(g, e, u):
                                 nc.vector.tensor_copy(plane, raw[g][:, t, :].indirect(picked))
                             else:
                                 nc.scalar.activation(plane, xb[g][:, t, :].indirect(picked), COPY)
-                for h in range(parts):
-                    if g == 0 and e < 2:
-                        grouped = early[:, e, :]
-                    else:
-                        grouped = keep.tile([P, width * 4], BF16, name="grouped%d_%d_%d" % (g, e, h), align_bytes=64)[:]
-                    nc.vector.tensor_copy(
-                        out=grouped.bitcast(F32).rearrange("p (n u) -> p n u", u=2),
-                        in_=halves[:].bitcast(F32)[:, :, h * width : (h + 1) * width].rearrange("p u n -> p n u"),
-                    )
-                    cols = slice(e * C + h * width, e * C + (h + 1) * width)
-                    nc.vector.quantize_mx(
-                        out=x_codes[g][:, cols].bitcast(FP8X4), scales=x_scales[g][:, cols], in_=grouped
-                    )
-                wcols = slice(g * N, (g + 1) * N)
+            for h in range(parts):
+                if k == 0:
+                    grouped = keep.tile([P, width * 4], BF16, name="grouped0", tag="raw1", align_bytes=64)
+                else:
+                    grouped = keep.tile([P, width * 4], BF16, name="grouped%d_%d" % (k, h), align_bytes=64)
+                nc.vector.tensor_copy(
+                    out=grouped[:].bitcast(F32).rearrange("p (c i u) -> p c u i", i=4, u=2),
+                    in_=halves[:].bitcast(F32)[:, :, h * width : (h + 1) * width].rearrange("p u (c i) -> p c u i", i=4),
+                )
+                cols = slice(base + h * width, base + (h + 1) * width)
+                nc.vector.quantize_mx(
+                    out=x_codes[g][:, cols].bitcast(FP8X4), scales=x_scales[g][:, cols], in_=grouped[:]
+                )
+            for e in experts:
+                wcols = slice((e % 2) * WE + g * N, (e % 2) * WE + (g + 1) * N)
                 for h in range(PARTS[e]):
                     cols = slice(e * C + h * (C // PARTS[e]), e * C + (h + 1) * (C // PARTS[e]))
                     nc.tensor.matmul_mx(
                         out=acc[e][h][:],
-                        lhsT=w_codes[e][:, wcols].bitcast(FP8X4),
-                        lhsT_scale=w_scales[e][:, wcols],
+                        lhsT=w_codes[e // 2][:, wcols].bitcast(FP8X4),
+                        lhsT_scale=w_scales[e // 2][:, wcols],
                         rhs=x_codes[g][:, cols].bitcast(FP8X4),
                         rhs_scale=x_scales[g][:, cols],
                         start=(g == 0),

@@ -36,7 +36,6 @@ def tile_routed_moe_kernel(tc, xT, w, gate, offs, pos1, pos2, out):
         offs_t = lists.tile([P, E * C // 16], U16, name="offs_t")
         pos1_t = lists.tile([P, T // 16], U16, name="pos1_t")
         pos2_t = lists.tile([P, T // 16], U16, name="pos2_t")
-        nc.sync.dma_start(offs_t[:], offs)
 
         warm_in = keep.tile([P, 1], F32, name="warm_in")
         warm_out = keep.tile([P, 1], F32, name="warm_out")
@@ -49,6 +48,8 @@ def tile_routed_moe_kernel(tc, xT, w, gate, offs, pos1, pos2, out):
             raw.append(keep.tile([P, 4, T], F32, name="raw%d" % g, tag="raw%d" % g, align_bytes=64))
             for t in range(4):
                 nc.sync.dma_start(raw[g][:, t, :], x_view[g, :, t, :])
+                if g == 0 and t == 0:
+                    nc.sync.dma_start(offs_t[:], offs)
         w_raw = []
         for h in range(E // 2):
             w_raw.append(keep.tile([P, 2 * PASSES, 4, N], F32, name="w_raw%d" % h))

@@ -18,12 +18,16 @@ COPY = mybir.ActivationFunctionType.Copy
 P = 128
 PASSES = K // 512
 
-UNITS = [(0, (0, 1), 1), (0, (2, 3), 1), (1, (0,), 1), (1, (1,), 1), (1, (2,), 1), (1, (3,), 2)]
+UNITS = [(0, (0, 1, 2, 3), 1), (1, (0, 1), 1), (1, (2,), 1), (1, (3,), 2)]
 PARTS = [1, 1, 1, 2]
+VECTOR_COPIES = [(2, 0)]
 
 
-def on_vector(g, e, u):
-    return e == 0 or (g == 0 and e == 1 and u == 1)
+SHARED = (0, 1, 0)
+
+
+def on_vector(g, e, u, h):
+    return e == 0 or (g == 0 and e == 1 and u == 1) or ((g, e, u) == SHARED and h == 0)
 
 
 def tile_routed_moe_kernel(tc, xT, w, gate, offs, pos1, pos2, out):
@@ -50,14 +54,12 @@ def tile_routed_moe_kernel(tc, xT, w, gate, offs, pos1, pos2, out):
                 nc.sync.dma_start(raw[g][:, t, :], x_view[g, :, t, :])
                 if g == 0 and t == 0:
                     nc.sync.dma_start(offs_t[:], offs)
-        w_raw = []
-        for h in range(E // 2):
-            w_raw.append(keep.tile([P, 2 * PASSES, 4, N], F32, name="w_raw%d" % h))
-            for j in range(2):
-                nc.sync.dma_start(
-                    w_raw[h][:, j * PASSES : (j + 1) * PASSES, :, :],
-                    w[2 * h + j].rearrange("(g p t) n -> p g t n", g=PASSES, p=P, t=4),
-                )
+        w_raw = keep.tile([P, E * PASSES, 4, N], F32, name="w_raw")
+        for e in range(E):
+            nc.sync.dma_start(
+                w_raw[:, e * PASSES : (e + 1) * PASSES, :, :],
+                w[e].rearrange("(g p t) n -> p g t n", g=PASSES, p=P, t=4),
+            )
         nc.sync.dma_start(pos1_t[:], pos1)
         nc.sync.dma_start(pos2_t[:], pos2)
         gate_t = []
@@ -66,37 +68,29 @@ def tile_routed_moe_kernel(tc, xT, w, gate, offs, pos1, pos2, out):
             nc.sync.dma_start(gate_t[r][:], gate[r])
 
         xb = [keep.tile([P, 4, T], BF16, name="xb0"), keep.tile([P, 4, T], BF16, name="xb1", tag="late")]
-        nc.vector.tensor_copy(out=xb[0][:, 0, :], in_=raw[0][:, 0, :])
+        nc.scalar.activation(xb[0][:, 0, :], raw[0][:, 0, :], COPY)
         for t in range(1, 4):
             nc.gpsimd.tensor_scalar(xb[0][:, t, :], raw[0][:, t, :], 1.0, 0.0, MULT, ADD)
         for u in range(2):
             nc.gpsimd.tensor_scalar(xb[1][:, 2 * u : 2 * u + 2, :], raw[1][:, 2 * u : 2 * u + 2, :], 1.0, 0.0, MULT, ADD)
 
         WE = PASSES * N
-        w_codes, w_scales = [], []
-        for h in range(E // 2):
-            w_grouped = keep.tile([P, 2 * WE * 4], BF16, name="w_grouped%d" % h, align_bytes=64)
-            w_codes.append(keep.tile([P, 2 * WE], U32, name="w_codes%d" % h, align_bytes=64))
-            w_scales.append(keep.tile([P, 2 * WE], U8, name="w_scales%d" % h, align_bytes=64))
-            if h == 0:
-                nc.gpsimd.tensor_scalar(
-                    w_grouped[:, 0 : WE * 4].rearrange("p (g n t) -> p g n t", g=PASSES, t=4),
-                    w_raw[h][:, 0:PASSES, :, :].rearrange("p g t n -> p g n t"),
-                    1.0,
-                    0.0,
-                    MULT,
-                    ADD,
-                )
-                nc.vector.tensor_copy(
-                    out=w_grouped[:, WE * 4 : 2 * WE * 4].rearrange("p (g c i t) -> p g c t i", g=PASSES, i=4, t=4),
-                    in_=w_raw[h][:, PASSES : 2 * PASSES, :, :].rearrange("p g t (c i) -> p g c t i", i=4),
-                )
-            else:
-                nc.vector.tensor_copy(
-                    out=w_grouped[:].rearrange("p (g c i t) -> p g c t i", g=2 * PASSES, i=4, t=4),
-                    in_=w_raw[h][:].rearrange("p g t (c i) -> p g c t i", i=4),
-                )
-            nc.vector.quantize_mx(out=w_codes[h][:].bitcast(FP8X4), scales=w_scales[h][:], in_=w_grouped[:])
+        w_grouped = keep.tile([P, E * WE * 4], BF16, name="w_grouped", align_bytes=64)
+        w_codes = keep.tile([P, E * WE], U32, name="w_codes", align_bytes=64)
+        w_scales = keep.tile([P, E * WE], U8, name="w_scales", align_bytes=64)
+        nc.gpsimd.tensor_scalar(
+            w_grouped[:, 0 : WE * 4].rearrange("p (g n t) -> p g n t", g=PASSES, t=4),
+            w_raw[:, 0:PASSES, :, :].rearrange("p g t n -> p g n t"),
+            1.0,
+            0.0,
+            MULT,
+            ADD,
+        )
+        nc.vector.tensor_copy(
+            out=w_grouped[:, WE * 4 :].rearrange("p (g c i t) -> p g c t i", g=(E - 1) * PASSES, i=4, t=4),
+            in_=w_raw[:, PASSES:, :, :].rearrange("p g t (c i) -> p g c t i", i=4),
+        )
+        nc.vector.quantize_mx(out=w_codes[:].bitcast(FP8X4), scales=w_scales[:], in_=w_grouped[:])
 
         x_codes = [keep.tile([P, E * C], U32, name="x_codes%d" % g, align_bytes=64) for g in range(PASSES)]
         x_scales = [keep.tile([P, E * C], U8, name="x_scales%d" % g, align_bytes=64) for g in range(PASSES)]
@@ -110,14 +104,15 @@ def tile_routed_moe_kernel(tc, xT, w, gate, offs, pos1, pos2, out):
             halves = keep.tile([P, 2, 2 * slots], BF16, name="halves%d" % k)
             for j, e in enumerate(experts):
                 for u in range(2):
-                    for h in range(parts if u == 1 else 1):
-                        n = C // parts if u == 1 else C
+                    pieces = 2 if (g, e, u) == SHARED else (parts if u == 1 else 1)
+                    for h in range(pieces):
+                        n = C // pieces
                         first_col = (e * C + h * n) // 16
                         picked = offs_t[:, first_col : first_col + n // 16]
                         for t in (2 * u, 2 * u + 1):
                             plane = halves[:, u, :].rearrange("p (n i) -> p n i", i=2)
                             plane = plane[:, j * C + h * n : j * C + (h + 1) * n, t % 2]
-                            if on_vector(g, e, u):
+                            if on_vector(g, e, u, h):
                                 nc.vector.tensor_copy(plane, raw[g][:, t, :].indirect(picked))
                             else:
                                 nc.scalar.activation(plane, xb[g][:, t, :].indirect(picked), COPY)
@@ -135,20 +130,23 @@ def tile_routed_moe_kernel(tc, xT, w, gate, offs, pos1, pos2, out):
                     out=x_codes[g][:, cols].bitcast(FP8X4), scales=x_scales[g][:, cols], in_=grouped[:]
                 )
             for e in experts:
-                wcols = slice((e % 2) * WE + g * N, (e % 2) * WE + (g + 1) * N)
+                wcols = slice(e * WE + g * N, e * WE + (g + 1) * N)
                 for h in range(PARTS[e]):
                     cols = slice(e * C + h * (C // PARTS[e]), e * C + (h + 1) * (C // PARTS[e]))
                     nc.tensor.matmul_mx(
                         out=acc[e][h][:],
-                        lhsT=w_codes[e // 2][:, wcols].bitcast(FP8X4),
-                        lhsT_scale=w_scales[e // 2][:, wcols],
+                        lhsT=w_codes[:, wcols].bitcast(FP8X4),
+                        lhsT_scale=w_scales[:, wcols],
                         rhs=x_codes[g][:, cols].bitcast(FP8X4),
                         rhs_scale=x_scales[g][:, cols],
                         start=(g == 0),
                         stop=(g == PASSES - 1),
                     )
-                    if g == PASSES - 1:
+                    if g == PASSES - 1 and (e, h) not in VECTOR_COPIES:
                         nc.scalar.copy(out=y_sb[:, cols], in_=acc[e][h][:])
+        for e, h in VECTOR_COPIES:
+            cols = slice(e * C + h * (C // PARTS[e]), e * C + (h + 1) * (C // PARTS[e]))
+            nc.vector.tensor_copy(out=y_sb[:, cols], in_=acc[e][h][:])
 
         first = keep.tile([P, T], F32, name="first")
         second = keep.tile([P, T], F32, name="second")

@@ -23,7 +23,7 @@ PARTS = [1, 1, 1, 2]
 VECTOR_COPIES = [(2, 0)]
 
 
-SHARED = (0, 1, 0)
+SHARED = (1, 3, 1)
 
 
 def on_vector(g, e, u, h):

@@ -150,10 +150,15 @@ def tile_routed_moe_kernel(tc, xT, w, gate, offs, pos1, pos2, out):
 
         first = keep.tile([P, T], F32, name="first")
         second = keep.tile([P, T], F32, name="second")
-        nc.vector.tensor_tensor(first[:], y_sb[:].indirect(pos1_t[:]), gate_t[0][:], MULT)
-        nc.vector.tensor_tensor(second[:], y_sb[:].indirect(pos2_t[:]), gate_t[1][:], MULT)
         result = keep.tile([P, T], F32, name="result")
+        H = T // 2
+        nc.vector.tensor_tensor(first[:], y_sb[:].indirect(pos1_t[:]), gate_t[0][:], MULT)
+        for h in range(2):
+            cols = slice(h * H, (h + 1) * H)
+            nc.vector.tensor_tensor(
+                second[:, cols], y_sb[:].indirect(pos2_t[:, h * H // 16 : (h + 1) * H // 16]), gate_t[1][:, cols], MULT
+            )
         for h, queue in enumerate((nc.sync, nc.scalar)):
-            cols = slice(h * T // 2, (h + 1) * T // 2)
+            cols = slice(h * H, (h + 1) * H)
             nc.vector.tensor_tensor(result[:, cols], first[:, cols], second[:, cols], ADD)
             queue.dma_start(out[:, cols], result[:, cols])

@@ -68,7 +68,8 @@ def tile_routed_moe_kernel(tc, xT, w, gate, offs, pos1, pos2, out):
             nc.sync.dma_start(gate_t[r][:], gate[r])
 
         xb = [keep.tile([P, 4, T], BF16, name="xb0"), keep.tile([P, 4, T], BF16, name="xb1", tag="late")]
-        nc.scalar.activation(xb[0][:, 0, :], raw[0][:, 0, :], COPY)
+        nc.scalar.activation(xb[0][:, 0, 0 : T // 2], raw[0][:, 0, 0 : T // 2], COPY)
+        nc.gpsimd.tensor_scalar(xb[0][:, 0, T // 2 :], raw[0][:, 0, T // 2 :], 1.0, 0.0, MULT, ADD)
         for t in range(1, 4):
             nc.gpsimd.tensor_scalar(xb[0][:, t, :], raw[0][:, t, :], 1.0, 0.0, MULT, ADD)
         for u in range(2):

@@ -159,7 +159,7 @@ def tile_routed_moe_kernel(tc, xT, w, gate, offs, pos1, pos2, out):
             nc.vector.tensor_tensor(
                 second[:, cols], y_sb[:].indirect(pos2_t[:, h * H // 16 : (h + 1) * H // 16]), gate_t[1][:, cols], MULT
             )
-        for h, queue in enumerate((nc.sync, nc.scalar)):
+        for h, queue in enumerate((nc.scalar, nc.scalar)):
             cols = slice(h * H, (h + 1) * H)
             nc.vector.tensor_tensor(result[:, cols], first[:, cols], second[:, cols], ADD)
             queue.dma_start(out[:, cols], result[:, cols])

@@ -88,8 +88,8 @@ def tile_routed_moe_kernel(tc, xT, w, gate, offs, pos1, pos2, out):
             ADD,
         )
         nc.vector.tensor_copy(
-            out=w_grouped[:, WE * 4 :].rearrange("p (g c i t) -> p g c t i", g=(E - 1) * PASSES, i=4, t=4),
-            in_=w_raw[:, PASSES:, :, :].rearrange("p g t (c i) -> p g c t i", i=4),
+            out=w_grouped[:, WE * 4 :].rearrange("p (g c i t) -> p g c t i", g=(E - 1) * PASSES, i=8, t=4),
+            in_=w_raw[:, PASSES:, :, :].rearrange("p g t (c i) -> p g c t i", i=8),
         )
         nc.vector.quantize_mx(out=w_codes[:].bitcast(FP8X4), scales=w_scales[:], in_=w_grouped[:])
 

from contextlib import ExitStack

import concourse.mybir as mybir

K, T, E, C, N = 1024, 512, 4, 256, 128
FLOPS = 2 * K * E * C * N

F32 = mybir.dt.float32
BF16 = mybir.dt.bfloat16
U32 = mybir.dt.uint32
U16 = mybir.dt.uint16
U8 = mybir.dt.uint8
FP8X4 = mybir.dt.float8_e4m3fn_x4
MULT = mybir.AluOpType.mult
ADD = mybir.AluOpType.add
COPY = mybir.ActivationFunctionType.Copy

P = 128
PASSES = K // 512

UNITS = [(0, (0, 1, 2, 3), 1), (1, (0, 1), 1), (1, (2,), 1), (1, (3,), 2)]
PARTS = [1, 1, 1, 2]
VECTOR_COPIES = [(2, 0)]


SHARED = (1, 3, 1)


def on_vector(g, e, u, h):
    return e == 0 or (g == 0 and e == 1 and u == 1) or ((g, e, u) == SHARED and h == 0)


def tile_routed_moe_kernel(tc, xT, w, gate, offs, pos1, pos2, out):
    nc = tc.nc
    with ExitStack() as ctx:
        lists = ctx.enter_context(tc.tile_pool(name="lists", bufs=1))
        keep = ctx.enter_context(tc.tile_pool(name="keep", bufs=1))
        psum = ctx.enter_context(tc.psum_pool(name="psum", bufs=1))

        offs_t = lists.tile([P, E * C // 16], U16, name="offs_t")
        pos1_t = lists.tile([P, T // 16], U16, name="pos1_t")
        pos2_t = lists.tile([P, T // 16], U16, name="pos2_t")

        warm_in = keep.tile([P, 1], F32, name="warm_in")
        warm_out = keep.tile([P, 1], F32, name="warm_out")
        nc.vector.memset(warm_in[:], 0.0)
        nc.scalar.activation(warm_out[:], warm_in[:], COPY)

        x_view = xT.rearrange("(g p t) n -> g p t n", g=PASSES, p=P, t=4)
        raw = []
        for g in range(PASSES):
            raw.append(keep.tile([P, 4, T], F32, name="raw%d" % g, tag="raw%d" % g, align_bytes=64))
            for t in range(4):
                nc.sync.dma_start(raw[g][:, t, :], x_view[g, :, t, :])
                if g == 0 and t == 0:
                    nc.sync.dma_start(offs_t[:], offs)
        w_raw = keep.tile([P, E * PASSES, 4, N], F32, name="w_raw")
        for e in range(E):
            nc.sync.dma_start(
                w_raw[:, e * PASSES : (e + 1) * PASSES, :, :],
                w[e].rearrange("(g p t) n -> p g t n", g=PASSES, p=P, t=4),
            )
        nc.sync.dma_start(pos1_t[:], pos1)
        nc.sync.dma_start(pos2_t[:], pos2)
        gate_t = []
        for r in range(2):
            gate_t.append(keep.tile([P, T], F32, name="gate%d" % r))
            nc.sync.dma_start(gate_t[r][:], gate[r])

        xb = [keep.tile([P, 4, T], BF16, name="xb0"), keep.tile([P, 4, T], BF16, name="xb1", tag="late")]
        nc.scalar.activation(xb[0][:, 0, 0 : T // 2], raw[0][:, 0, 0 : T // 2], COPY)
        nc.gpsimd.tensor_scalar(xb[0][:, 0, T // 2 :], raw[0][:, 0, T // 2 :], 1.0, 0.0, MULT, ADD)
        for t in range(1, 4):
            nc.gpsimd.tensor_scalar(xb[0][:, t, :], raw[0][:, t, :], 1.0, 0.0, MULT, ADD)
        for u in range(2):
            nc.gpsimd.tensor_scalar(xb[1][:, 2 * u : 2 * u + 2, :], raw[1][:, 2 * u : 2 * u + 2, :], 1.0, 0.0, MULT, ADD)

        WE = PASSES * N
        w_grouped = keep.tile([P, E * WE * 4], BF16, name="w_grouped", align_bytes=64)
        w_codes = keep.tile([P, E * WE], U32, name="w_codes", align_bytes=64)
        w_scales = keep.tile([P, E * WE], U8, name="w_scales", align_bytes=64)
        nc.gpsimd.tensor_scalar(
            w_grouped[:, 0 : WE * 4].rearrange("p (g n t) -> p g n t", g=PASSES, t=4),
            w_raw[:, 0:PASSES, :, :].rearrange("p g t n -> p g n t"),
            1.0,
            0.0,
            MULT,
            ADD,
        )
        nc.vector.tensor_copy(
            out=w_grouped[:, WE * 4 :].rearrange("p (g c i t) -> p g c t i", g=(E - 1) * PASSES, i=8, t=4),
            in_=w_raw[:, PASSES:, :, :].rearrange("p g t (c i) -> p g c t i", i=8),
        )
        nc.vector.quantize_mx(out=w_codes[:].bitcast(FP8X4), scales=w_scales[:], in_=w_grouped[:])

        x_codes = [keep.tile([P, E * C], U32, name="x_codes%d" % g, align_bytes=64) for g in range(PASSES)]
        x_scales = [keep.tile([P, E * C], U8, name="x_scales%d" % g, align_bytes=64) for g in range(PASSES)]
        acc = [[psum.tile([P, C // PARTS[e]], F32, name="acc%d_%d" % (e, h)) for h in range(PARTS[e])] for e in range(E)]
        y_sb = keep.tile([P, E * C], F32, name="y_sb", tag="late")

        for k, (g, experts, parts) in enumerate(UNITS):
            slots = C * len(experts)
            width = slots // parts
            base = experts[0] * C
            halves = keep.tile([P, 2, 2 * slots], BF16, name="halves%d" % k)
            for j, e in enumerate(experts):
                for u in range(2):
                    pieces = 2 if (g, e, u) == SHARED else (parts if u == 1 else 1)
                    for h in range(pieces):
                        n = C // pieces
                        first_col = (e * C + h * n) // 16
                        picked = offs_t[:, first_col : first_col + n // 16]
                        for t in (2 * u, 2 * u + 1):
                            plane = halves[:, u, :].rearrange("p (n i) -> p n i", i=2)
                            plane = plane[:, j * C + h * n : j * C + (h + 1) * n, t % 2]
                            if on_vector(g, e, u, h):
                                nc.vector.tensor_copy(plane, raw[g][:, t, :].indirect(picked))
                            else:
                                nc.scalar.activation(plane, xb[g][:, t, :].indirect(picked), COPY)
            for h in range(parts):
                if k == 0:
                    grouped = keep.tile([P, width * 4], BF16, name="grouped0", tag="raw1", align_bytes=64)
                else:
                    grouped = keep.tile([P, width * 4], BF16, name="grouped%d_%d" % (k, h), align_bytes=64)
                nc.vector.tensor_copy(
                    out=grouped[:].bitcast(F32).rearrange("p (c i u) -> p c u i", i=4, u=2),
                    in_=halves[:].bitcast(F32)[:, :, h * width : (h + 1) * width].rearrange("p u (c i) -> p c u i", i=4),
                )
                cols = slice(base + h * width, base + (h + 1) * width)
                nc.vector.quantize_mx(
                    out=x_codes[g][:, cols].bitcast(FP8X4), scales=x_scales[g][:, cols], in_=grouped[:]
                )
            for e in experts:
                wcols = slice(e * WE + g * N, e * WE + (g + 1) * N)
                for h in range(PARTS[e]):
                    cols = slice(e * C + h * (C // PARTS[e]), e * C + (h + 1) * (C // PARTS[e]))
                    nc.tensor.matmul_mx(
                        out=acc[e][h][:],
                        lhsT=w_codes[:, wcols].bitcast(FP8X4),
                        lhsT_scale=w_scales[:, wcols],
                        rhs=x_codes[g][:, cols].bitcast(FP8X4),
                        rhs_scale=x_scales[g][:, cols],
                        start=(g == 0),
                        stop=(g == PASSES - 1),
                    )
                    if g == PASSES - 1 and (e, h) not in VECTOR_COPIES:
                        nc.scalar.copy(out=y_sb[:, cols], in_=acc[e][h][:])
        for e, h in VECTOR_COPIES:
            cols = slice(e * C + h * (C // PARTS[e]), e * C + (h + 1) * (C // PARTS[e]))
            nc.vector.tensor_copy(out=y_sb[:, cols], in_=acc[e][h][:])

        first = keep.tile([P, T], F32, name="first")
        second = keep.tile([P, T], F32, name="second")
        result = keep.tile([P, T], F32, name="result")
        H = T // 2
        nc.vector.tensor_tensor(first[:], y_sb[:].indirect(pos1_t[:]), gate_t[0][:], MULT)
        for h in range(2):
            cols = slice(h * H, (h + 1) * H)
            nc.vector.tensor_tensor(
                second[:, cols], y_sb[:].indirect(pos2_t[:, h * H // 16 : (h + 1) * H // 16]), gate_t[1][:, cols], MULT
            )
        for h, queue in enumerate((nc.scalar, nc.scalar)):
            cols = slice(h * H, (h + 1) * H)
            nc.vector.tensor_tensor(result[:, cols], first[:, cols], second[:, cols], ADD)
            queue.dma_start(out[:, cols], result[:, cols])
